import numpy as np
CORES = [2,10,18,26,34,42,50,58,66,74,82,90,98,106,114,122,130,138,146,154,162,170,178,186,194,202,210,218,226,234,242,250]
N = 32
GROUPS = [[0,16],[1,17],[2,18],[3,19],[4,20],[5,21],[6,22],[7,23],[8,24],[9,25],[10,26],[11,27],[12,28],[13,29],[14,30],[15,31]]
def setup_inputs(rng):
    return {"x": rng.standard_normal((N, 128, 16), dtype=np.float32)}
def reference(x):
    y = np.empty((N, 128, 16), x.dtype)
    for g in GROUPS:
        s = x[g].max(axis=0)
        for r in g:
            y[r] = s
    return {"y": y}

from concourse.bass import DstId, RemoteDMATransfer

SCRATCH = {
    "xs": ("dram", [128, 16], "float32"),
    "land": ("dram", [2, 128, 16], "float32"),
    "res": ("dram", [128, 16], "float32"),
}
SEMAPHORES = ["loaded", "sent", "arrived", "stored"]

HELPER_OFFSET = 1
OFF_CHIP_ENGINES = 0x00FF
ON_CHIP_ENGINES = 0xFF00
MAX = 2


def _dst(topo, dst, src):
    rid, pid = topo.addr(dst, src)
    return DstId(rid=rid, pnc=pid)


def rank_program(g, core, T, topo):
    rank = T.rank_of(core)
    if rank is not None:
        group = [m for m in T.tables["GROUPS"] if rank in m][0]
        slot = group.index(rank)
        partner = T.cores[group[1 - slot]]
        g.sync.dma_start(T.xs[:], T.x[:]).then_inc(T.sem.loaded, 16)
        g.wait_ge(T.sem.loaded, 16)
        g.remote_dma_fused(
            [
                RemoteDMATransfer(dst_ids=[_dst(topo, partner + HELPER_OFFSET, core)],
                                  dma_engine_mask=OFF_CHIP_ENGINES, remote_sem=T.sem.arrived,
                                  src=T.xs[:], dst=T.land[slot]),
                RemoteDMATransfer(dst_ids=[_dst(topo, core + HELPER_OFFSET, core)],
                                  dma_engine_mask=ON_CHIP_ENGINES, remote_sem=T.sem.arrived,
                                  src=T.xs[:], dst=T.land[slot]),
            ],
            local_sem=T.sem.sent,
        )
        g.sync.wait_ge(T.sem.arrived, 16)
        g.sync.dma_start(T.y[:], T.res[:]).then_inc(T.sem.stored, 16)
        g.wait_ge(T.sem.sent, 16)
        g.sync.wait_ge(T.sem.stored, 16)
        return

    owner = core - HELPER_OFFSET
    if owner >= 0 and T.rank_of(owner) is not None:
        g.wait_ge(T.sem.arrived, 16)
        g.remote_dma_fused(
            [
                RemoteDMATransfer(dst_ids=[_dst(topo, owner, core)], dma_engine_mask=0xFFFF,
                                  remote_sem=T.sem.arrived, srcs=[T.land[0], T.land[1]], dsts=[T.res[:]],
                                  alu_op=MAX),
            ],
            local_sem=T.sem.sent,
        )
        g.wait_ge(T.sem.sent, 16)
